import numpy as np, ml_dtypes
CORES = [36,164,52,180,100,228,116,244]
N = 8
BF = ml_dtypes.bfloat16
def f(rng, *shape):
    return (rng.standard_normal(shape, dtype=np.float32) * np.exp2(rng.integers(-2, 3, shape[:-1] + (1,)))).astype(BF)
def wide(rng, *shape):
    v = f(rng, *shape).astype(np.float32); k = shape[:-2] + (1, shape[-1])
    return (v * np.exp2(rng.integers(-6, 7, k)) * (rng.random(k) > 0.0625)).astype(BF)
def gentries(a):
    return np.ascontiguousarray(a.reshape(8, 16, -1).transpose(0, 2, 1)).reshape(8, -1)
def gtable(e):
    e = np.asarray(e); return np.ascontiguousarray(e.reshape(8, -1, 16).transpose(0, 2, 1)).reshape(128, -1).astype(np.int32)
Q, CAPP, M, E, D = 128, 32, 2048, 4096, 4
LV, L = [1, 7, 90, 800], 1800
EMPTY = 2 ** 24 - 1
def cut(rng, n, m, cap, s):
    u = rng.random((m, cap - 1)) + s * rng.random((m, 1))
    return 1 + np.bincount(np.argsort(u.reshape(-1))[:n - m] // (cap - 1), minlength=m)
def tree(rng, lv, n, keys, repeat=False):
    nk = np.sort(rng.integers(0, EMPTY - 16, (16, M)), axis=0) + np.arange(16)[:, None]
    nk[np.arange(16)[:, None] >= rng.integers(1, 17, (1, M))] = EMPTY
    beg = rng.integers(0, E - 15, M); kid = rng.integers(0, M, E)
    ids = np.concatenate([[0], 1 + rng.permutation(M - 1)]); a = np.cumsum([0] + list(lv))
    lev = [ids[a[l]:a[l + 1]] for l in range(D)]; nxt = lev[1:] + [rng.integers(0, M, n) if repeat else rng.permutation(M)[:n]]
    ek = np.asarray(keys); sizes = []
    for l in range(D - 1, -1, -1):
        sz = cut(rng, len(ek), lv[l], 16, 2.0); st = np.cumsum(sz) - sz
        nk[:, lev[l]] = EMPTY; nk[np.arange(len(ek)) - np.repeat(st, sz), np.repeat(lev[l], sz)] = ek
        ek = ek[st]; sizes.insert(0, sz)
    S = np.concatenate(sizes); C = np.concatenate(nxt); t = len(C); m = len(S)
    o = rng.permutation(m); so = S[o]; st = np.zeros(m, np.int64)
    st[o] = np.cumsum(so) - so + np.sort(rng.integers(0, E - 16 - t + 1, m))
    beg[ids[:m]] = st; kid[np.repeat(st - (np.cumsum(S) - S), S) + np.arange(t)] = C
    return nk, beg, kid
def make(rng, shapes=None, ends=False, full=False, alike=False, repeat=False):
    shapes = shapes or [(LV, L)] * N; I = np.int32
    spl = np.sort(rng.integers(0, EMPTY - 16384 * N + 1, (8, N - 1)), axis=1) + 16384 * np.arange(1, N)
    spl = np.concatenate([np.zeros((8, 1), np.int64), spl], axis=1); hi = np.concatenate([spl[:, 1:], np.full((8, 1), EMPTY)], axis=1)
    nk = np.zeros((N, 128, M), I); beg = np.zeros((N, 8, M), I); kid = np.zeros((N, 8, E), I); sk = np.zeros((N, 8, M), np.int64); ln = np.array([n for _, n in shapes])
    for r in range(N):
        lv, n = shapes[r]
        for g in range(8):
            w = int(hi[g, r] - spl[g, r])
            if ends: k = np.arange(n) + (w - n) * (r % 2)
            else: k = np.sort(rng.integers(0, w - n + 1, n)) + np.arange(n)
            k[0] = 0; k = k + spl[g, r]; sk[r, g, :n] = k
            nk[r, 16 * g:16 * g + 16], beg[r, g], kid[r, g] = tree(rng, lv, n, k, repeat)
    q = np.zeros((N, 8, Q), np.int64)
    for r in range(N):
        for g in range(8):
            if full: cn = np.zeros(N, np.int64); cn[rng.permutation(N)] = np.clip(Q - CAPP * np.arange(N), 0, CAPP)
            else: cn = 3 + cut(rng, Q - 3 * N, N, CAPP - 3, 0.5)
            own = np.repeat(np.arange(N), cn); st = np.cumsum(cn) - cn; occ = np.arange(Q) - st[own]
            a = spl[g, own]; b = hi[g, own]; k = sk[own, g, np.floor(rng.random(Q) * ln[own]).astype(np.int64)]
            inside = a + np.floor(rng.random(Q) * (b - a)).astype(np.int64)
            kd = 1 + occ % 4 if ends else np.array([0, 0, 0, 0, 0, 1, 1, 1, 2, 2, 2, 3, 4])[rng.integers(0, 13, Q)]
            v = np.choose(kd, [inside, k, np.maximum(k - 1, a), a, b - 1])
            if alike: v = v[st[own]]
            q[r, g] = v[rng.permutation(Q)]
    return {"nk": nk, "beg": beg, "kid": kid, "vec": f(rng, N, 128, M), "spl": np.stack([spl.astype(I)] * N), "q": np.stack([gtable(x) for x in q])}
def setup_inputs(rng):
    return make(rng)
def setup_inputs_caps(rng):
    return make(rng, full=True)
def setup_inputs_ends(rng):
    return make(rng, ends=True)
def setup_inputs_shapes(rng):
    a = []; n = M
    for l in range(D): n = -(-n // 16); a.insert(0, n)
    k = M * 3 // 8; b = [min(16 ** l, k) for l in range(D)]; s = int(rng.integers(0, 2))
    return make(rng, shapes=[(a, M) if (r + s) % 2 else (b, k) for r in range(N)], repeat=True)
def setup_inputs_alike(rng):
    return make(rng, alike=True)
def setup_inputs_spread(rng):
    d = make(rng); d["vec"] = wide(rng, N, 128, M); return d
def check_inputs(d):
    bad = []; nk, beg, kid, spl, q = [np.asarray(d[x]).astype(np.int64) for x in ("nk", "beg", "kid", "spl", "q")]
    if not np.isfinite(np.asarray(d["vec"]).astype(np.float32)).all(): bad.append("finite")
    if any(bool((a < 0).any() or (a > b).any()) for a, b in ((nk, EMPTY), (beg, E - 16), (kid, M - 1), (spl, EMPTY - 1), (q, EMPTY - 1))): return bad + ["ranges"]
    if (spl != spl[:1]).any() or (spl[:, :, 0] != 0).any() or (np.diff(spl, axis=2) <= 0).any(): return bad + ["splitters"]
    n4 = nk.reshape(N, 8, 16, M)
    if ((n4[:, :, 1:] <= n4[:, :, :-1]) & (n4[:, :, 1:] < EMPTY)).any(): bad.append("nodes")
    ok = True
    for r in range(N):
        for g in range(8):
            nd = np.zeros(1, np.int64); ek = spl[r, g, r:r + 1]; seen = [nd]
            for l in range(D):
                k = n4[r, g][:, nd].T
                if len(nd) > M or (k[:, 0] != ek).any(): ok = False; break
                use = k < EMPTY; ek = k[use]; nd = kid[r, g][(beg[r, g][nd][:, None] + np.arange(16))[use]]
                if l < D - 1:
                    seen.append(nd)
                    if len(nd) > M: ok = False; break
            if not ok: break
            s = np.concatenate(seen); top = spl[r, g, r + 1] if r + 1 < N else EMPTY
            if len(np.unique(s)) != len(s) or (np.diff(ek) <= 0).any() or ek[-1] >= top: ok = False
        if not ok: break
    if not ok: bad.append("tree")
    for r in range(N):
        x = gentries(q[r]); own = np.sum(x[:, :, None] >= spl[r][:, None, :], axis=2) - 1
        if any(np.bincount(own[g], minlength=N).max() > CAPP for g in range(8)): bad.append("caps"); break
    return bad
def reference(nk, beg, kid, vec, spl, q):
    y = np.zeros((N, 128, Q), vec.dtype); G = np.arange(8)[:, None]
    n4 = nk.reshape(N, 8, 16, M); v4 = vec.reshape(N, 8, 16, M)
    for r in range(N):
        x = gentries(q[r])
        own = np.sum(x[:, :, None] >= spl[r][:, None, :], axis=2) - 1
        at = np.zeros((8, Q), np.int64)
        for l in range(D):
            c = np.sum(n4[own, G, :, at] <= x[:, :, None], axis=2)
            at = kid[own, G, beg[own, G, at] + c - 1]
        y[r] = v4[own, G, :, at].transpose(0, 2, 1).reshape(128, Q)
    return {"y": y}

@@ -1,0 +1,294 @@
+from concourse.bass import DstId, RemoteDMATransfer
+from concourse.mybir import AluOpType as Op, ActivationFunctionType as Act
+
+N = 8
+NEV = 130
+PART = ((0, 5), (5, 8))
+
+SCRATCH = {
+    "xq": ("sbuf", [128, 128], "int32"),
+    "splc": ("sbuf", [128, 1], "int32"),
+    "splf": ("sbuf", [128, 1], "float32"),
+    "pidx": ("sbuf", [128, 1], "int32"),
+    "pand": ("sbuf", [128, 1], "int32"),
+    "init": ("sbuf", [128, 1], "float32"),
+    "zer": ("sbuf", [128, 128], "float32"),
+    "ge0": ("sbuf", [128, 128], "float16"),
+    "cnt": ("sbuf", [128, 128], "float32"),
+    "pslot": ("sbuf", [128, 128], "float16"),
+    "tslot": ("sbuf", [128, 4, 32], "float32"),
+    "lslot": ("sbuf", [128, 8], "uint16"),
+    "tback": ("sbuf", [128, 32], "float32"),
+    "lback": ("sbuf", [128, 8], "uint16"),
+    "xs": ("sbuf", [128, 256], "float32"),
+    "cst": ("sbuf", [128, 528], "float32"),
+    "csh": ("sbuf", [128, 528], "float16"),
+    "kids": ("sbuf", [128, 4096], "int32"),
+    "begi": ("sbuf", [128, 128], "int32"),
+    "begl": ("sbuf", [128, 128], "uint16"),
+    "ckr0": ("sbuf", [128, 1024], "float16"),
+    "ckr1": ("sbuf", [128, 1024], "float16"),
+    "dck": ("sbuf", [128, 2048], "float32"),
+    "nkt": ("sbuf", [128, 2048], "int32"),
+    "nk0": ("sbuf", [128, 1], "float32"),
+    "vect": ("sbuf", [128, 2048], "bfloat16"),
+    "xr": ("sbuf", [128, 256], "float32"),
+    "ans0": ("sbuf", [128, 160], "bfloat16"),
+    "ans1": ("sbuf", [128, 96], "bfloat16"),
+    "ar": ("sbuf", [128, 256], "bfloat16"),
+    "ysb": ("sbuf", [128, 128], "bfloat16"),
+    "pse": ("psum", [128, 512], "float32"),
+    "ps0": ("psum", [128, 16, 32], "float32"),
+    "ps1": ("psum", [128, 16, 32], "float32"),
+}
+for _q in range(4):
+    SCRATCH["pd%d" % _q] = ("psum", [128, 512], "float32")
+for _h in range(2):
+    _n = PART[_h][1] - PART[_h][0]
+    for _l in range(1, 5):
+        SCRATCH["g%d_%d" % (_h, _l)] = ("sbuf", [128, 32 * _n], "float16")
+        SCRATCH["p%d_%d" % (_h, _l)] = ("sbuf", [128, 32 * _n], "float16")
+        SCRATCH["t%d_%d" % (_h, _l)] = ("sbuf", [128, _n, 32], "float32")
+        SCRATCH["l%d_%d" % (_h, _l)] = ("sbuf", [128, 2 * _n], "uint16")
+
+SEMAPHORES = ["qa", "qb", "qs", "ra", "rs", "xin", "kin", "gate"] + ["e%d" % i for i in range(NEV)]
+
+
+def rank_program(g, core, T, topo):
+    me = T.rank_of(core)
+    if me is None:
+        return
+    V, S, P, Y = g.vector, g.scalar, g.tensor, g.sync
+    used = [0]
+    open_events = {}
+
+    def mark(inst, n=1):
+        i = used[0]
+        used[0] += 1
+        inst.then_inc(T.sem["e%d" % i], n)
+        open_events[i] = n
+        return i, n
+
+    def need(queue, *events):
+        for i, n in events:
+            queue.wait_ge(T.sem["e%d" % i], n)
+            open_events.pop(i, None)
+
+    Y.dma_start(T.splc[0:128:2, 0:1], T.spl[:, :]).then_inc(T.sem.xin, 16)
+    S.dma_start(T.splc[1:128:2, 0:1], T.spl[:, :]).then_inc(T.sem.xin, 16)
+    for o in range(16):
+        (Y, S)[o % 2].dma_start(T.xq[o:128:16, :], T.q[:, :]).then_inc(T.sem.xin, 16)
+    XIN = 18 * 16
+    e_beg = mark(Y.dma_start(T.begi[:, :], T.beg[:, :]), 16)
+    for o in range(16):
+        (S, Y)[o % 2].dma_start(T.kids[o:128:16, 0:4081], T.kid[:, o:o + 4081]).then_inc(T.sem.kin, 16)
+    KIN = 16 * 16
+    Y.wait_ge(T.sem.gate, 1)
+    e_nk = mark(Y.dma_start(T.nkt[:, :], T.nk[:, :]), 16)
+    e_vec = mark(Y.dma_start(T.vect[:, :], T.vec[:, :]), 16)
+
+    e_z = mark(V.memset(T.cst[:, :], 0.0))
+    e_zer = mark(V.memset(T.zer[:, :], 0.0))
+    e_xs0 = mark(V.memset(T.xs[:, :], 0.0))
+    e_pi = mark(g.iota(T.pidx[:, :], [[0, 1]], 0, 1))
+    need(g, e_z)
+
+    def sel(ap, pattern, cmp, fill, base, cm):
+        return mark(g.affine_select(ap, ap, pattern, cmp, fill, base, cm))
+
+    a0, a1 = T.cst[:, 8:136:32], T.cst[:, 144:272:32]
+    e1 = sel(T.cst[:, 272:400:2], [[-2, 64]], Op.not_equal, 1.0, 0, 1)
+    e2 = sel(a0, [[32, 4]], Op.is_gt, 1.0, 0, -1)
+    e3 = sel(a1, [[32, 4]], Op.is_gt, 1.0, 16, -1)
+    e4 = sel(T.cst[:, 400:528], [[-1, 128]], Op.not_equal, -1.0, 1, 1)
+    need(g, e1)
+    e1 = sel(T.cst[:, 272:400:2], [[-2, 64]], Op.not_equal, -1.0, -2, 1)
+    need(g, e2)
+    e2 = sel(a0, [[32, 4]], Op.is_ge, 0.0, 15, -1)
+    need(g, e3)
+    e3 = sel(a1, [[32, 4]], Op.is_ge, 0.0, 31, -1)
+    need(g, e4)
+    e4 = sel(T.cst[:, 400:528:16], [[-16, 8]], Op.not_equal, 0.0, 1, 1)
+    need(g, e1)
+    e1 = sel(T.cst[:, 286:400:16], [[-16, 8]], Op.not_equal, 0.0, -16, 1)
+    need(g, e4)
+    e4 = sel(T.cst[:, 400:528], [[-1, 128]], Op.not_equal, 1.0, 0, 1)
+    need(V, e_pi)
+    e_pa = mark(V.tensor_scalar(T.pand[:, :], T.pidx[:, :], 15, None, Op.bitwise_and))
+    need(V, e_pa)
+    e_init = mark(V.tensor_scalar(T.init[:, :], T.pand[:, :], 16.0, -1.0, Op.mult, Op.add))
+    need(V, e1, e2, e3, e4)
+    e_c = mark(V.tensor_copy(T.csh[:, :], T.cst[:, :]))
+    dm, dd = T.csh[:, 272:400], T.csh[:, 400:528]
+
+    def lay(par, c):
+        return T.csh[:, 136 * par + 8 - c:136 * par + 136 - c]
+
+    def lists(ps, n, src):
+        for par in range(2):
+            out = ps[:, 0:n, 16 * par:16 * par + 16]
+            P.matmul(out, lay(par, 0), src[:, 0:16 * n], True, False)
+            last = P.matmul(out, lay(par, 1), src[:, 16 * n:32 * n], False, True)
+        return mark(last)
+
+    def narrow(lst, n, t):
+        return [mark(V.tensor_copy(lst[:, n * c:n * c + n], t[:, :, c])) for c in range(2)]
+
+    V.wait_ge(T.sem.xin, XIN)
+    e_sf = mark(V.tensor_copy(T.splf[:, :], T.splc[:, :]))
+    need(V, e_sf)
+    e = mark(V.tensor_scalar(T.ge0[:, :], T.xq[:, :], T.splf[:, 0:1], None, Op.is_ge))
+    need(P, e_c, e)
+    e_e = mark(P.matmul(T.pse[:, 0:128], dm, T.ge0[:, :], True, True))
+    need(V, e_zer, e_init, e_e)
+    e = mark(V.tensor_tensor_scan(T.cnt[:, :], T.pse[:, 0:128], T.zer[:, :], T.init[:, 0:1], Op.add, Op.add))
+    need(V, e)
+    e_p = mark(V.tensor_tensor(T.pslot[:, :], T.cnt[:, :], T.pse[:, 0:128], Op.mult))
+    need(P, e_p)
+    e = lists(T.ps0, 4, T.pslot)
+    need(V, e)
+    e = mark(V.transpose(T.tslot[:, :, :], T.ps0[:, 0:4, :]))
+    need(V, e)
+    es = narrow(T.lslot, 4, T.tslot)
+    need(V, e_xs0, *es)
+    e_x = mark(V.tensor_copy(T.xs[:, 0:256].indirect(T.lslot[:, 0:8]), T.xq[:, :]))
+
+    W = len(topo.engines(core, T.cores[(me + 1) % N])) // 4
+
+    def send(ks, make, sem):
+        tr = []
+        for i, k in enumerate(ks):
+            src, dst, to = make(k)
+            c = T.cores[to]
+            rid, pnc = topo.addr(c, core)
+            m = 0
+            for x in topo.engines(core, c)[W * i:W * i + W]:
+                m |= 1 << x
+            tr.append(RemoteDMATransfer(src=src, dst=dst, dst_ids=[DstId(rid=rid, pnc=pnc)], dma_engine_mask=m,
+                                        remote_sem=sem))
+        return tr
+
+    def to_owner(k):
+        d = (me + k) % N
+        return T.xs[:, 32 * d:32 * d + 32], T.xr[:, 32 * k:32 * k + 32], d
+
+    need(g, e_x)
+    g.remote_dma_fused(send((1, 2, 3, 4), to_owner, T.sem.qa), local_sem=T.sem.qs)
+    g.remote_dma_fused(send((5, 6, 7), to_owner, T.sem.qb), local_sem=T.sem.qs)
+    g.sem_inc(T.sem.gate, 1)
+
+    need(V, e_x)
+    e_own = mark(V.tensor_copy(T.xr[:, 0:32], T.xs[:, 32 * me:32 * me + 32]))
+
+    for par in range(2):
+        for b in range(8):
+            last = P.matmul(T.ps1[:, 0, 16 * par:16 * par + 16], lay(par, b), T.pslot[:, b:128:8], b == 0, b == 7)
+    e_lb = mark(last)
+
+    need(V, e_beg)
+    e_bl = mark(V.tensor_copy(T.begl[:, :], T.begi[:, :]))
+    need(V, e_lb)
+    e = mark(V.transpose(T.tback[:, :], T.ps1[:, 0, :]))
+    need(V, e)
+    e_lback = mark(V.tensor_copy(T.lback[:, :], T.tback[:, 0:8]))
+    need(V, e_bl)
+    V.wait_ge(T.sem.kin, KIN)
+    e_k = [mark(V.tensor_copy(T["ckr%d" % h][:, :], T.kids[:, 0:4081].indirect(T.begl[:, 64 * h:64 * h + 64])))
+           for h in range(2)]
+    e_d = []
+    for h in range(2):
+        need(P, e_k[h])
+        for a in range(16):
+            c0 = 128 * (a % 4) + 64 * h
+            last = P.matmul(T["pd%d" % (a // 4)][:, c0:c0 + 64], dd, T["ckr%d" % h][:, a:1024:16], True, True)
+            if h and a % 4 == 3:
+                e_d.append(mark(last))
+    e_t = []
+    for q in range(4):
+        src, dst = T["pd%d" % q][:, :], T.dck[:, 512 * q:512 * q + 512]
+        if q % 2 == 0:
+            need(S, e_d[q])
+            e_t.append(mark(S.activation(dst, src, Act.Copy)))
+        else:
+            need(V, e_d[q])
+            e_t.append(mark(V.tensor_copy(dst, src)))
+    need(V, e_nk)
+    e_n0 = mark(V.tensor_copy(T.nk0[:, :], T.nkt[:, 0:1]))
+    need(V, e_n0, *e_t)
+
+    last_list = [[], []]
+    e_sum = [None, None]
+
+    def find(h, l):
+        b0, b1 = PART[h]
+        x = T.xr[:, 32 * b0:32 * b1]
+        p = T["p%d_%d" % (h, l)]
+        if l == 1:
+            if h == 0:
+                need(V, e_own)
+                V.wait_ge(T.sem.qa, 4 * W)
+            else:
+                V.wait_ge(T.sem.qb, 3 * W)
+            e = mark(V.tensor_scalar(p[:, :], x, T.nk0[:, 0:1], T.dck[:, 0:1], Op.is_ge, Op.mult))
+        else:
+            lst = T["l%d_%d" % (h, l - 1)][:, :]
+            need(V, *last_list[h])
+            e = mark(V.tensor_tensor(T["g%d_%d" % (h, l)][:, :], T.nkt[:, 0:2048].indirect(lst), x, Op.is_le))
+            need(V, e)
+            e = mark(V.tensor_tensor(p[:, :], T.dck[:, 0:2048].indirect(lst), T["g%d_%d" % (h, l)][:, :], Op.mult))
+        need(P, e)
+        e_sum[h] = lists(T["ps%d" % h], b1 - b0, p)
+
+    def turn(h, l):
+        t = T["t%d_%d" % (h, l)]
+        n = PART[h][1] - PART[h][0]
+        need(V, e_sum[h])
+        e = mark(V.transpose(t[:, :, :], T["ps%d" % h][:, 0:n, :]))
+        need(V, e)
+        last_list[h] = narrow(T["l%d_%d" % (h, l)], n, t)
+
+    def to_asker(k):
+        h = 0 if k < PART[0][1] else 1
+        c = 32 * (k - PART[h][0])
+        return T["ans%d" % h][:, c:c + 32], T.ar[:, 32 * me:32 * me + 32], (me - k) % N
+
+    def answer(h):
+        if h == 0:
+            need(V, e_vec)
+        need(V, *last_list[h])
+        e = mark(V.tensor_copy(T["ans%d" % h][:, :], T.vect[:, 0:2048].indirect(T["l%d_4" % h][:, :])))
+        need(g, e)
+        g.remote_dma_fused(send(((1, 2, 3, 4), (5, 6, 7))[h], to_asker, T.sem.ra), local_sem=T.sem.rs)
+        return e
+
+    find(0, 1)
+    turn(0, 1)
+    find(0, 2)
+    find(1, 1)
+    turn(0, 2)
+    turn(1, 1)
+    find(0, 3)
+    find(1, 2)
+    turn(0, 3)
+    turn(1, 2)
+    find(0, 4)
+    find(1, 3)
+    turn(0, 4)
+    e_a = answer(0)
+    turn(1, 3)
+    find(1, 4)
+    turn(1, 4)
+    answer(1)
+
+    need(V, e_a)
+    e = mark(V.tensor_copy(T.ar[:, 32 * me:32 * me + 32], T.ans0[:, 0:32]))
+    need(V, e, e_lback)
+    V.wait_ge(T.sem.ra, 7 * W)
+    e = mark(V.tensor_copy(T.ysb[:, :], T.ar[:, 0:256].indirect(T.lback[:, 0:8])))
+    need(Y, e)
+    e = mark(Y.dma_start(T.y[:, :], T.ysb[:, :]), 16)
+    need(Y, e)
+    g.wait_ge(T.sem.qs, 7 * W)
+    g.wait_ge(T.sem.rs, 7 * W)
+    for i in sorted(open_events):
+        need(g, (i, open_events[i]))

@@ -3,7 +3,7 @@ from concourse.mybir import AluOpType as Op, ActivationFunctionType as Act
 
 N = 8
 NEV = 130
-PART = ((0, 5), (5, 8))
+HALF = ((1, 2, 3, 4), (5, 6, 7))
 
 SCRATCH = {
     "xq": ("sbuf", [128, 128], "int32"),
@@ -30,11 +30,12 @@ SCRATCH = {
     "ckr1": ("sbuf", [128, 1024], "float16"),
     "dck": ("sbuf", [128, 2048], "float32"),
     "nkt": ("sbuf", [128, 2048], "int32"),
+    "nkc": ("sbuf", [128, 8], "int32"),
     "nk0": ("sbuf", [128, 1], "float32"),
     "vect": ("sbuf", [128, 2048], "bfloat16"),
     "xr": ("sbuf", [128, 256], "float32"),
-    "ans0": ("sbuf", [128, 160], "bfloat16"),
-    "ans1": ("sbuf", [128, 96], "bfloat16"),
+    "ans0": ("sbuf", [128, 128], "bfloat16"),
+    "ans1": ("sbuf", [128, 128], "bfloat16"),
     "ar": ("sbuf", [128, 256], "bfloat16"),
     "ysb": ("sbuf", [128, 128], "bfloat16"),
     "pse": ("psum", [128, 512], "float32"),
@@ -44,14 +45,13 @@ SCRATCH = {
 for _q in range(4):
     SCRATCH["pd%d" % _q] = ("psum", [128, 512], "float32")
 for _h in range(2):
-    _n = PART[_h][1] - PART[_h][0]
     for _l in range(1, 5):
-        SCRATCH["g%d_%d" % (_h, _l)] = ("sbuf", [128, 32 * _n], "float16")
-        SCRATCH["p%d_%d" % (_h, _l)] = ("sbuf", [128, 32 * _n], "float16")
-        SCRATCH["t%d_%d" % (_h, _l)] = ("sbuf", [128, _n, 32], "float32")
-        SCRATCH["l%d_%d" % (_h, _l)] = ("sbuf", [128, 2 * _n], "uint16")
+        SCRATCH["g%d_%d" % (_h, _l)] = ("sbuf", [128, 128], "float16")
+        SCRATCH["p%d_%d" % (_h, _l)] = ("sbuf", [128, 128], "float16")
+        SCRATCH["t%d_%d" % (_h, _l)] = ("sbuf", [128, 4, 32], "float32")
+        SCRATCH["l%d_%d" % (_h, _l)] = ("sbuf", [128, 8], "uint16")
 
-SEMAPHORES = ["qa", "qb", "qs", "ra", "rs", "xin", "kin", "gate"] + ["e%d" % i for i in range(NEV)]
+SEMAPHORES = ["qa", "qb", "qs", "ra", "rs", "sin", "xin", "kin", "gate"] + ["e%d" % i for i in range(NEV)]
 
 
 def rank_program(g, core, T, topo):
@@ -74,15 +74,14 @@ def rank_program(g, core, T, topo):
             queue.wait_ge(T.sem["e%d" % i], n)
             open_events.pop(i, None)
 
-    Y.dma_start(T.splc[0:128:2, 0:1], T.spl[:, :]).then_inc(T.sem.xin, 16)
-    S.dma_start(T.splc[1:128:2, 0:1], T.spl[:, :]).then_inc(T.sem.xin, 16)
+    Y.dma_start(T.splc[0:128:2, 0:1], T.spl[:, :]).then_inc(T.sem.sin, 16)
+    S.dma_start(T.splc[1:128:2, 0:1], T.spl[:, :]).then_inc(T.sem.sin, 16)
     for o in range(16):
         (Y, S)[o % 2].dma_start(T.xq[o:128:16, :], T.q[:, :]).then_inc(T.sem.xin, 16)
-    XIN = 18 * 16
     e_beg = mark(Y.dma_start(T.begi[:, :], T.beg[:, :]), 16)
     for o in range(16):
         (S, Y)[o % 2].dma_start(T.kids[o:128:16, 0:4081], T.kid[:, o:o + 4081]).then_inc(T.sem.kin, 16)
-    KIN = 16 * 16
+    e_nkc = mark(Y.dma_start(T.nkc[:, :], T.nk[:, 0:8]), 16)
     Y.wait_ge(T.sem.gate, 1)
     e_nk = mark(Y.dma_start(T.nkt[:, :], T.nk[:, :]), 16)
     e_vec = mark(Y.dma_start(T.vect[:, :], T.vec[:, :]), 16)
@@ -124,19 +123,20 @@ def rank_program(g, core, T, topo):
     def lay(par, c):
         return T.csh[:, 136 * par + 8 - c:136 * par + 136 - c]
 
-    def lists(ps, n, src):
+    def lists(ps, src):
         for par in range(2):
-            out = ps[:, 0:n, 16 * par:16 * par + 16]
-            P.matmul(out, lay(par, 0), src[:, 0:16 * n], True, False)
-            last = P.matmul(out, lay(par, 1), src[:, 16 * n:32 * n], False, True)
+            out = ps[:, 0:4, 16 * par:16 * par + 16]
+            P.matmul(out, lay(par, 0), src[:, 0:64], True, False)
+            last = P.matmul(out, lay(par, 1), src[:, 64:128], False, True)
         return mark(last)
 
-    def narrow(lst, n, t):
-        return [mark(V.tensor_copy(lst[:, n * c:n * c + n], t[:, :, c])) for c in range(2)]
+    def narrow(lst, t):
+        return [mark(V.tensor_copy(lst[:, 4 * c:4 * c + 4], t[:, :, c])) for c in range(2)]
 
-    V.wait_ge(T.sem.xin, XIN)
+    V.wait_ge(T.sem.sin, 2 * 16)
     e_sf = mark(V.tensor_copy(T.splf[:, :], T.splc[:, :]))
     need(V, e_sf)
+    V.wait_ge(T.sem.xin, 16 * 16)
     e = mark(V.tensor_scalar(T.ge0[:, :], T.xq[:, :], T.splf[:, 0:1], None, Op.is_ge))
     need(P, e_c, e)
     e_e = mark(P.matmul(T.pse[:, 0:128], dm, T.ge0[:, :], True, True))
@@ -145,11 +145,13 @@ def rank_program(g, core, T, topo):
     need(V, e)
     e_p = mark(V.tensor_tensor(T.pslot[:, :], T.cnt[:, :], T.pse[:, 0:128], Op.mult))
     need(P, e_p)
-    e = lists(T.ps0, 4, T.pslot)
+    e = lists(T.ps0, T.pslot)
+    need(V, e_beg)
+    e_bl = mark(V.tensor_copy(T.begl[:, :], T.begi[:, :]))
     need(V, e)
     e = mark(V.transpose(T.tslot[:, :, :], T.ps0[:, 0:4, :]))
     need(V, e)
-    es = narrow(T.lslot, 4, T.tslot)
+    es = narrow(T.lslot, T.tslot)
     need(V, e_xs0, *es)
     e_x = mark(V.tensor_copy(T.xs[:, 0:256].indirect(T.lslot[:, 0:8]), T.xq[:, :]))
 
@@ -170,119 +172,105 @@ def rank_program(g, core, T, topo):
 
     def to_owner(k):
         d = (me + k) % N
-        return T.xs[:, 32 * d:32 * d + 32], T.xr[:, 32 * k:32 * k + 32], d
+        return T.xs[:, 32 * d:32 * d + 32], T.xr[:, 32 * k - 32:32 * k], d
 
     need(g, e_x)
-    g.remote_dma_fused(send((1, 2, 3, 4), to_owner, T.sem.qa), local_sem=T.sem.qs)
-    g.remote_dma_fused(send((5, 6, 7), to_owner, T.sem.qb), local_sem=T.sem.qs)
+    g.remote_dma_fused(send(HALF[0], to_owner, T.sem.qa), local_sem=T.sem.qs)
     g.sem_inc(T.sem.gate, 1)
+    g.remote_dma_fused(send(HALF[1], to_owner, T.sem.qb), local_sem=T.sem.qs)
 
-    need(V, e_x)
-    e_own = mark(V.tensor_copy(T.xr[:, 0:32], T.xs[:, 32 * me:32 * me + 32]))
+    need(S, e_x)
+    e_own = mark(S.activation(T.xr[:, 224:256], T.xs[:, 32 * me:32 * me + 32], Act.Copy))
 
     for par in range(2):
         for b in range(8):
-            last = P.matmul(T.ps1[:, 0, 16 * par:16 * par + 16], lay(par, b), T.pslot[:, b:128:8], b == 0, b == 7)
+            last = P.matmul(T.pse[:, 256 + 16 * par:272 + 16 * par], lay(par, b), T.pslot[:, b:128:8], b == 0, b == 7)
     e_lb = mark(last)
 
-    need(V, e_beg)
-    e_bl = mark(V.tensor_copy(T.begl[:, :], T.begi[:, :]))
-    need(V, e_lb)
-    e = mark(V.transpose(T.tback[:, :], T.ps1[:, 0, :]))
-    need(V, e)
-    e_lback = mark(V.tensor_copy(T.lback[:, :], T.tback[:, 0:8]))
     need(V, e_bl)
-    V.wait_ge(T.sem.kin, KIN)
+    V.wait_ge(T.sem.kin, 16 * 16)
     e_k = [mark(V.tensor_copy(T["ckr%d" % h][:, :], T.kids[:, 0:4081].indirect(T.begl[:, 64 * h:64 * h + 64])))
            for h in range(2)]
+    need(P, e_k[0])
+    e_d0 = mark(P.matmul(T.pse[:, 320:321], dd, T.ckr0[:, 0:1], True, True))
     e_d = []
     for h in range(2):
-        need(P, e_k[h])
+        if h:
+            need(P, e_k[1])
         for a in range(16):
             c0 = 128 * (a % 4) + 64 * h
             last = P.matmul(T["pd%d" % (a // 4)][:, c0:c0 + 64], dd, T["ckr%d" % h][:, a:1024:16], True, True)
             if h and a % 4 == 3:
                 e_d.append(mark(last))
     e_t = []
-    for q in range(4):
-        src, dst = T["pd%d" % q][:, :], T.dck[:, 512 * q:512 * q + 512]
-        if q % 2 == 0:
-            need(S, e_d[q])
-            e_t.append(mark(S.activation(dst, src, Act.Copy)))
-        else:
-            need(V, e_d[q])
-            e_t.append(mark(V.tensor_copy(dst, src)))
-    need(V, e_nk)
-    e_n0 = mark(V.tensor_copy(T.nk0[:, :], T.nkt[:, 0:1]))
-    need(V, e_n0, *e_t)
+    for q in range(3):
+        need(S, e_d[q])
+        e_t.append(mark(S.activation(T.dck[:, 512 * q:512 * q + 512], T["pd%d" % q][:, :], Act.Copy)))
+    need(V, e_nkc)
+    e_n0 = mark(V.tensor_copy(T.nk0[:, :], T.nkc[:, 0:1]))
 
-    last_list = [[], []]
-    e_sum = [None, None]
-
-    def find(h, l):
-        b0, b1 = PART[h]
-        x = T.xr[:, 32 * b0:32 * b1]
-        p = T["p%d_%d" % (h, l)]
+    need(V, e_n0, e_d0)
+    lst = [None, None]
+    e_l = [[], []]
+    for l in range(1, 5):
+        p = [T["p%d_%d" % (h, l)] for h in range(2)]
+        x = [T.xr[:, 128 * h:128 * h + 128] for h in range(2)]
+        e_m = []
         if l == 1:
-            if h == 0:
-                need(V, e_own)
-                V.wait_ge(T.sem.qa, 4 * W)
-            else:
-                V.wait_ge(T.sem.qb, 3 * W)
-            e = mark(V.tensor_scalar(p[:, :], x, T.nk0[:, 0:1], T.dck[:, 0:1], Op.is_ge, Op.mult))
+            for h in range(2):
+                if h == 0:
+                    V.wait_ge(T.sem.qa, 4 * W)
+                else:
+                    need(V, e_own)
+                    V.wait_ge(T.sem.qb, 3 * W)
+                e_m.append(mark(V.tensor_scalar(p[h][:, :], x[h], T.nk0[:, 0:1], T.pse[:, 320:321], Op.is_ge, Op.mult)))
         else:
-            lst = T["l%d_%d" % (h, l - 1)][:, :]
-            need(V, *last_list[h])
-            e = mark(V.tensor_tensor(T["g%d_%d" % (h, l)][:, :], T.nkt[:, 0:2048].indirect(lst), x, Op.is_le))
-            need(V, e)
-            e = mark(V.tensor_tensor(p[:, :], T.dck[:, 0:2048].indirect(lst), T["g%d_%d" % (h, l)][:, :], Op.mult))
-        need(P, e)
-        e_sum[h] = lists(T["ps%d" % h], b1 - b0, p)
-
-    def turn(h, l):
-        t = T["t%d_%d" % (h, l)]
-        n = PART[h][1] - PART[h][0]
-        need(V, e_sum[h])
-        e = mark(V.transpose(t[:, :, :], T["ps%d" % h][:, 0:n, :]))
-        need(V, e)
-        last_list[h] = narrow(T["l%d_%d" % (h, l)], n, t)
+            if l == 2:
+                need(V, e_nk)
+            e_g = []
+            for h in range(2):
+                need(V, *e_l[h])
+                e_g.append(mark(V.tensor_tensor(T["g%d_%d" % (h, l)][:, :], T.nkt[:, 0:2048].indirect(lst[h]), x[h], Op.is_le)))
+            if l == 2:
+                need(V, *e_t)
+            for h in range(2):
+                need(V, e_g[h])
+                e_m.append(mark(V.tensor_tensor(p[h][:, :], T.dck[:, 0:2048].indirect(lst[h]),
+                                                T["g%d_%d" % (h, l)][:, :], Op.mult)))
+        e_s = []
+        for h in range(2):
+            need(P, e_m[h])
+            e_s.append(lists(T["ps%d" % h], p[h]))
+        if l == 1:
+            need(V, e_d[3])
+            e_t.append(mark(V.tensor_copy(T.dck[:, 1536:2048], T.pd3[:, :])))
+        e_r = []
+        for h in range(2):
+            need(V, e_s[h])
+            e_r.append(mark(V.transpose(T["t%d_%d" % (h, l)][:, :, :], T["ps%d" % h][:, 0:4, :])))
+        for h in range(2):
+            need(V, e_r[h])
+            e_l[h] = narrow(T["l%d_%d" % (h, l)], T["t%d_%d" % (h, l)])
+            lst[h] = T["l%d_%d" % (h, l)][:, :]
 
     def to_asker(k):
-        h = 0 if k < PART[0][1] else 1
-        c = 32 * (k - PART[h][0])
+        h, c = (k - 1) // 4, 32 * ((k - 1) % 4)
         return T["ans%d" % h][:, c:c + 32], T.ar[:, 32 * me:32 * me + 32], (me - k) % N
 
-    def answer(h):
-        if h == 0:
-            need(V, e_vec)
-        need(V, *last_list[h])
-        e = mark(V.tensor_copy(T["ans%d" % h][:, :], T.vect[:, 0:2048].indirect(T["l%d_4" % h][:, :])))
-        need(g, e)
-        g.remote_dma_fused(send(((1, 2, 3, 4), (5, 6, 7))[h], to_asker, T.sem.ra), local_sem=T.sem.rs)
-        return e
+    need(V, e_vec)
+    for h in range(2):
+        need(V, *e_l[h])
+        e_a = mark(V.tensor_copy(T["ans%d" % h][:, :], T.vect[:, 0:2048].indirect(lst[h])))
+        need(g, e_a)
+        g.remote_dma_fused(send(HALF[h], to_asker, T.sem.ra), local_sem=T.sem.rs)
+    need(S, e_a)
+    e_ar = mark(S.activation(T.ar[:, 32 * me:32 * me + 32], T.ans1[:, 96:128], Act.Copy))
 
-    find(0, 1)
-    turn(0, 1)
-    find(0, 2)
-    find(1, 1)
-    turn(0, 2)
-    turn(1, 1)
-    find(0, 3)
-    find(1, 2)
-    turn(0, 3)
-    turn(1, 2)
-    find(0, 4)
-    find(1, 3)
-    turn(0, 4)
-    e_a = answer(0)
-    turn(1, 3)
-    find(1, 4)
-    turn(1, 4)
-    answer(1)
-
-    need(V, e_a)
-    e = mark(V.tensor_copy(T.ar[:, 32 * me:32 * me + 32], T.ans0[:, 0:32]))
-    need(V, e, e_lback)
+    need(V, e_lb)
+    e = mark(V.transpose(T.tback[:, :], T.pse[:, 256:288]))
+    need(V, e)
+    e = mark(V.tensor_copy(T.lback[:, :], T.tback[:, 0:8]))
+    need(V, e, e_ar)
     V.wait_ge(T.sem.ra, 7 * W)
     e = mark(V.tensor_copy(T.ysb[:, :], T.ar[:, 0:256].indirect(T.lback[:, 0:8])))
     need(Y, e)

@@ -21,8 +21,12 @@ SCRATCH = {
     "tback": ("sbuf", [128, 32], "float32"),
     "lback": ("sbuf", [128, 8], "uint16"),
     "xs": ("sbuf", [128, 256], "float32"),
-    "cst": ("sbuf", [128, 528], "float32"),
-    "csh": ("sbuf", [128, 528], "float16"),
+    "cdm": ("sbuf", [128, 128], "float32"),
+    "clay": ("sbuf", [128, 272], "float32"),
+    "cdd": ("sbuf", [128, 128], "float32"),
+    "hdm": ("sbuf", [128, 128], "float16"),
+    "hlay": ("sbuf", [128, 272], "float16"),
+    "hdd": ("sbuf", [128, 128], "float16"),
     "kids": ("sbuf", [128, 4096], "int32"),
     "begi": ("sbuf", [128, 128], "int32"),
     "begl": ("sbuf", [128, 128], "uint16"),
@@ -86,42 +90,47 @@ def rank_program(g, core, T, topo):
     e_nk = mark(Y.dma_start(T.nkt[:, :], T.nk[:, :]), 16)
     e_vec = mark(Y.dma_start(T.vect[:, :], T.vec[:, :]), 16)
 
-    e_z = mark(V.memset(T.cst[:, :], 0.0))
+    e_z1 = mark(V.memset(T.cdm[:, :], 0.0))
+    e_z2 = mark(V.memset(T.clay[:, :], 0.0))
+    e_z3 = mark(V.memset(T.cdd[:, :], 0.0))
     e_zer = mark(V.memset(T.zer[:, :], 0.0))
     e_xs0 = mark(V.memset(T.xs[:, :], 0.0))
-    e_pi = mark(g.iota(T.pidx[:, :], [[0, 1]], 0, 1))
-    need(g, e_z)
 
     def sel(ap, pattern, cmp, fill, base, cm):
         return mark(g.affine_select(ap, ap, pattern, cmp, fill, base, cm))
 
-    a0, a1 = T.cst[:, 8:136:32], T.cst[:, 144:272:32]
-    e1 = sel(T.cst[:, 272:400:2], [[-2, 64]], Op.not_equal, 1.0, 0, 1)
+    a0, a1 = T.clay[:, 8:136:32], T.clay[:, 144:272:32]
+    need(g, e_z1)
+    e1 = sel(T.cdm[:, 0:128:2], [[-2, 64]], Op.not_equal, 1.0, 0, 1)
+    need(g, e_z2)
     e2 = sel(a0, [[32, 4]], Op.is_gt, 1.0, 0, -1)
-    e3 = sel(a1, [[32, 4]], Op.is_gt, 1.0, 16, -1)
-    e4 = sel(T.cst[:, 400:528], [[-1, 128]], Op.not_equal, -1.0, 1, 1)
     need(g, e1)
-    e1 = sel(T.cst[:, 272:400:2], [[-2, 64]], Op.not_equal, -1.0, -2, 1)
+    e1 = sel(T.cdm[:, 0:128:2], [[-2, 64]], Op.not_equal, -1.0, -2, 1)
+    e3 = sel(a1, [[32, 4]], Op.is_gt, 1.0, 16, -1)
+    need(g, e1)
+    e1 = sel(T.cdm[:, 14:128:16], [[-16, 8]], Op.not_equal, 0.0, -16, 1)
+    e_pi = mark(g.iota(T.pidx[:, :], [[0, 1]], 0, 1))
     need(g, e2)
     e2 = sel(a0, [[32, 4]], Op.is_ge, 0.0, 15, -1)
     need(g, e3)
     e3 = sel(a1, [[32, 4]], Op.is_ge, 0.0, 31, -1)
+    need(g, e_z3)
+    e4 = sel(T.cdd[:, :], [[-1, 128]], Op.not_equal, -1.0, 1, 1)
     need(g, e4)
-    e4 = sel(T.cst[:, 400:528:16], [[-16, 8]], Op.not_equal, 0.0, 1, 1)
-    need(g, e1)
-    e1 = sel(T.cst[:, 286:400:16], [[-16, 8]], Op.not_equal, 0.0, -16, 1)
+    e4 = sel(T.cdd[:, 0:128:16], [[-16, 8]], Op.not_equal, 0.0, 1, 1)
     need(g, e4)
-    e4 = sel(T.cst[:, 400:528], [[-1, 128]], Op.not_equal, 1.0, 0, 1)
+    e4 = sel(T.cdd[:, :], [[-1, 128]], Op.not_equal, 1.0, 0, 1)
+    need(V, e1)
+    e_dm = mark(V.tensor_copy(T.hdm[:, :], T.cdm[:, :]))
     need(V, e_pi)
     e_pa = mark(V.tensor_scalar(T.pand[:, :], T.pidx[:, :], 15, None, Op.bitwise_and))
     need(V, e_pa)
     e_init = mark(V.tensor_scalar(T.init[:, :], T.pand[:, :], 16.0, -1.0, Op.mult, Op.add))
-    need(V, e1, e2, e3, e4)
-    e_c = mark(V.tensor_copy(T.csh[:, :], T.cst[:, :]))
-    dm, dd = T.csh[:, 272:400], T.csh[:, 400:528]
+    need(V, e2, e3)
+    e_lay = mark(V.tensor_copy(T.hlay[:, :], T.clay[:, :]))
 
     def lay(par, c):
-        return T.csh[:, 136 * par + 8 - c:136 * par + 136 - c]
+        return T.hlay[:, 136 * par + 8 - c:136 * par + 136 - c]
 
     def lists(ps, src):
         for par in range(2):
@@ -138,14 +147,16 @@ def rank_program(g, core, T, topo):
     need(V, e_sf)
     V.wait_ge(T.sem.xin, 16 * 16)
     e = mark(V.tensor_scalar(T.ge0[:, :], T.xq[:, :], T.splf[:, 0:1], None, Op.is_ge))
-    need(P, e_c, e)
-    e_e = mark(P.matmul(T.pse[:, 0:128], dm, T.ge0[:, :], True, True))
+    need(P, e_dm, e)
+    e_e = mark(P.matmul(T.pse[:, 0:128], T.hdm[:, :], T.ge0[:, :], True, True))
     need(V, e_zer, e_init, e_e)
     e = mark(V.tensor_tensor_scan(T.cnt[:, :], T.pse[:, 0:128], T.zer[:, :], T.init[:, 0:1], Op.add, Op.add))
     need(V, e)
     e_p = mark(V.tensor_tensor(T.pslot[:, :], T.cnt[:, :], T.pse[:, 0:128], Op.mult))
-    need(P, e_p)
+    need(P, e_lay, e_p)
     e = lists(T.ps0, T.pslot)
+    need(V, e4)
+    e_dd = mark(V.tensor_copy(T.hdd[:, :], T.cdd[:, :]))
     need(V, e_beg)
     e_bl = mark(V.tensor_copy(T.begl[:, :], T.begi[:, :]))
     need(V, e)
@@ -191,15 +202,15 @@ def rank_program(g, core, T, topo):
     V.wait_ge(T.sem.kin, 16 * 16)
     e_k = [mark(V.tensor_copy(T["ckr%d" % h][:, :], T.kids[:, 0:4081].indirect(T.begl[:, 64 * h:64 * h + 64])))
            for h in range(2)]
-    need(P, e_k[0])
-    e_d0 = mark(P.matmul(T.pse[:, 320:321], dd, T.ckr0[:, 0:1], True, True))
+    need(P, e_dd, e_k[0])
+    e_d0 = mark(P.matmul(T.pse[:, 320:321], T.hdd[:, :], T.ckr0[:, 0:1], True, True))
     e_d = []
     for h in range(2):
         if h:
             need(P, e_k[1])
         for a in range(16):
             c0 = 128 * (a % 4) + 64 * h
-            last = P.matmul(T["pd%d" % (a // 4)][:, c0:c0 + 64], dd, T["ckr%d" % h][:, a:1024:16], True, True)
+            last = P.matmul(T["pd%d" % (a // 4)][:, c0:c0 + 64], T.hdd[:, :], T["ckr%d" % h][:, a:1024:16], True, True)
             if h and a % 4 == 3:
                 e_d.append(mark(last))
     e_t = []

@@ -6,26 +6,29 @@ NEV = 130
 HALF = ((1, 2, 3, 4), (5, 6, 7))
 
 SCRATCH = {
-    "xq": ("sbuf", [128, 128], "int32"),
+    "xc": ("sbuf", [128, 128], "int32"),
+    "q8": ("sbuf", [128, 128], "int32"),
+    "q8f": ("sbuf", [128, 128], "float32"),
+    "xq": ("sbuf", [128, 128], "float32"),
     "splc": ("sbuf", [128, 1], "int32"),
     "splf": ("sbuf", [128, 1], "float32"),
-    "pidx": ("sbuf", [128, 1], "int32"),
     "pand": ("sbuf", [128, 1], "int32"),
     "init": ("sbuf", [128, 1], "float32"),
-    "zer": ("sbuf", [128, 128], "float32"),
-    "ge0": ("sbuf", [128, 128], "float16"),
+    "ge0": ("sbuf", [128, 128], "bfloat16"),
     "cnt": ("sbuf", [128, 128], "float32"),
-    "pslot": ("sbuf", [128, 128], "float16"),
+    "pslot": ("sbuf", [128, 128], "bfloat16"),
     "tslot": ("sbuf", [128, 4, 32], "float32"),
     "lslot": ("sbuf", [128, 8], "uint16"),
     "tback": ("sbuf", [128, 32], "float32"),
     "lback": ("sbuf", [128, 8], "uint16"),
     "xs": ("sbuf", [128, 256], "float32"),
-    "cdm": ("sbuf", [128, 128], "float32"),
-    "clay": ("sbuf", [128, 272], "float32"),
-    "cdd": ("sbuf", [128, 128], "float32"),
-    "hdm": ("sbuf", [128, 128], "float16"),
-    "hlay": ("sbuf", [128, 272], "float16"),
+    "pg": ("sbuf", [128, 128], "int32"),
+    "rep": ("sbuf", [128, 128], "float32"),
+    "bdm": ("sbuf", [128, 64], "bfloat16"),
+    "bsl": ("sbuf", [128, 264], "bfloat16"),
+    "blay": ("sbuf", [128, 264], "bfloat16"),
+    "bdd": ("sbuf", [128, 128], "bfloat16"),
+    "hlay": ("sbuf", [128, 264], "float16"),
     "hdd": ("sbuf", [128, 128], "float16"),
     "kids": ("sbuf", [128, 4096], "int32"),
     "begi": ("sbuf", [128, 128], "int32"),
@@ -43,6 +46,7 @@ SCRATCH = {
     "ar": ("sbuf", [128, 256], "bfloat16"),
     "ysb": ("sbuf", [128, 128], "bfloat16"),
     "pse": ("psum", [128, 512], "float32"),
+    "psx": ("psum", [128, 512], "float32"),
     "ps0": ("psum", [128, 16, 32], "float32"),
     "ps1": ("psum", [128, 16, 32], "float32"),
 }
@@ -55,7 +59,7 @@ for _h in range(2):
         SCRATCH["t%d_%d" % (_h, _l)] = ("sbuf", [128, 4, 32], "float32")
         SCRATCH["l%d_%d" % (_h, _l)] = ("sbuf", [128, 8], "uint16")
 
-SEMAPHORES = ["qa", "qb", "qs", "ra", "rs", "sin", "xin", "kin", "gate"] + ["e%d" % i for i in range(NEV)]
+SEMAPHORES = ["qa", "qb", "qs", "ra", "rs", "sin", "cin", "kin", "gate"] + ["e%d" % i for i in range(NEV)]
 
 
 def rank_program(g, core, T, topo):
@@ -78,10 +82,10 @@ def rank_program(g, core, T, topo):
             queue.wait_ge(T.sem["e%d" % i], n)
             open_events.pop(i, None)
 
-    Y.dma_start(T.splc[0:128:2, 0:1], T.spl[:, :]).then_inc(T.sem.sin, 16)
-    S.dma_start(T.splc[1:128:2, 0:1], T.spl[:, :]).then_inc(T.sem.sin, 16)
-    for o in range(16):
-        (Y, S)[o % 2].dma_start(T.xq[o:128:16, :], T.q[:, :]).then_inc(T.sem.xin, 16)
+    S.dma_start(T.splc[0:64, 0:1], T.spl[:, :]).then_inc(T.sem.sin, 16)
+    for r in range(N):
+        (Y, S)[r % 2].dma_start(T.xc[r:64:8, :], T.q[:, :]).then_inc(T.sem.cin, 16)
+    e_q8 = mark(Y.dma_start(T.q8[0:8, :], T.q[:, :]), 16)
     e_beg = mark(Y.dma_start(T.begi[:, :], T.beg[:, :]), 16)
     for o in range(16):
         (S, Y)[o % 2].dma_start(T.kids[o:128:16, 0:4081], T.kid[:, o:o + 4081]).then_inc(T.sem.kin, 16)
@@ -90,80 +94,85 @@ def rank_program(g, core, T, topo):
     e_nk = mark(Y.dma_start(T.nkt[:, :], T.nk[:, :]), 16)
     e_vec = mark(Y.dma_start(T.vect[:, :], T.vec[:, :]), 16)
 
-    e_z1 = mark(V.memset(T.cdm[:, :], 0.0))
-    e_z2 = mark(V.memset(T.clay[:, :], 0.0))
-    e_z3 = mark(V.memset(T.cdd[:, :], 0.0))
-    e_zer = mark(V.memset(T.zer[:, :], 0.0))
+    e_z1 = mark(V.memset(T.bdm[0:64, :], 0.0))
+    e_z2 = mark(V.memset(T.bsl[:, :], 0.0))
+    e_z3 = mark(V.memset(T.bdd[:, :], 0.0))
+    e_z4 = mark(V.memset(T.blay[:, :], 0.0))
     e_xs0 = mark(V.memset(T.xs[:, :], 0.0))
 
     def sel(ap, pattern, cmp, fill, base, cm):
         return mark(g.affine_select(ap, ap, pattern, cmp, fill, base, cm))
 
-    a0, a1 = T.clay[:, 8:136:32], T.clay[:, 144:272:32]
+    e_pg = mark(g.iota(T.pg[:, :], [[-1, 8], [0, 16]], 0, 1))
     need(g, e_z1)
-    e1 = sel(T.cdm[:, 0:128:2], [[-2, 64]], Op.not_equal, 1.0, 0, 1)
+    e1 = sel(T.bdm[0:64, :], [[-1, 64]], Op.not_equal, -1.0, -1, 1)
+    need(g, e1)
+    e1 = sel(T.bdm[0:64, 7:64:8], [[-8, 8]], Op.not_equal, 0.0, -8, 1)
+    need(g, e1)
+    e_dm = sel(T.bdm[0:64, :], [[-1, 64]], Op.not_equal, 1.0, 0, 1)
     need(g, e_z2)
-    e2 = sel(a0, [[32, 4]], Op.is_gt, 1.0, 0, -1)
-    need(g, e1)
-    e1 = sel(T.cdm[:, 0:128:2], [[-2, 64]], Op.not_equal, -1.0, -2, 1)
-    e3 = sel(a1, [[32, 4]], Op.is_gt, 1.0, 16, -1)
-    need(g, e1)
-    e1 = sel(T.cdm[:, 14:128:16], [[-16, 8]], Op.not_equal, 0.0, -16, 1)
-    e_pi = mark(g.iota(T.pidx[:, :], [[0, 1]], 0, 1))
+    e2 = sel(T.bsl[:, 8:264:32], [[8, 2], [16, 4]], Op.is_gt, 1.0, 0, -1)
     need(g, e2)
-    e2 = sel(a0, [[32, 4]], Op.is_ge, 0.0, 15, -1)
-    need(g, e3)
-    e3 = sel(a1, [[32, 4]], Op.is_ge, 0.0, 31, -1)
+    e_sl = sel(T.bsl[:, 8:264:32], [[8, 2], [16, 4]], Op.is_ge, 0.0, 7, -1)
     need(g, e_z3)
-    e4 = sel(T.cdd[:, :], [[-1, 128]], Op.not_equal, -1.0, 1, 1)
+    e4 = sel(T.bdd[:, :], [[-1, 128]], Op.not_equal, -1.0, 1, 1)
     need(g, e4)
-    e4 = sel(T.cdd[:, 0:128:16], [[-16, 8]], Op.not_equal, 0.0, 1, 1)
+    e4 = sel(T.bdd[:, 0:128:16], [[-16, 8]], Op.not_equal, 0.0, 1, 1)
     need(g, e4)
-    e4 = sel(T.cdd[:, :], [[-1, 128]], Op.not_equal, 1.0, 0, 1)
-    need(V, e1)
-    e_dm = mark(V.tensor_copy(T.hdm[:, :], T.cdm[:, :]))
-    need(V, e_pi)
-    e_pa = mark(V.tensor_scalar(T.pand[:, :], T.pidx[:, :], 15, None, Op.bitwise_and))
+    e4 = sel(T.bdd[:, :], [[-1, 128]], Op.not_equal, 1.0, 0, 1)
+    need(g, e_z4)
+    e5 = sel(T.blay[:, 8:264:32], [[16, 2], [32, 4]], Op.is_gt, 1.0, 0, -1)
+    need(g, e5)
+    e_lay = sel(T.blay[:, 8:264:32], [[16, 2], [32, 4]], Op.is_ge, 0.0, 15, -1)
+    need(V, e_pg)
+    e_rep = mark(V.tensor_scalar(T.rep[:, :], T.pg[:, :], 0.0, None, Op.is_equal))
+    e_pa = mark(V.tensor_scalar(T.pand[0:64, :], T.pg[0:64, 0:1], 7, None, Op.bitwise_and))
     need(V, e_pa)
-    e_init = mark(V.tensor_scalar(T.init[:, :], T.pand[:, :], 16.0, -1.0, Op.mult, Op.add))
-    need(V, e2, e3)
-    e_lay = mark(V.tensor_copy(T.hlay[:, :], T.clay[:, :]))
+    e_init = mark(V.tensor_scalar(T.init[0:64, :], T.pand[0:64, :], 32.0, -1.0, Op.mult, Op.add))
 
-    def lay(par, c):
-        return T.hlay[:, 136 * par + 8 - c:136 * par + 136 - c]
+    def lay(m, par, c):
+        return m[:, 128 * par + 8 - c:128 * par + 136 - c]
 
-    def lists(ps, src):
+    def lists(m, ps, src):
         for par in range(2):
             out = ps[:, 0:4, 16 * par:16 * par + 16]
-            P.matmul(out, lay(par, 0), src[:, 0:64], True, False)
-            last = P.matmul(out, lay(par, 1), src[:, 64:128], False, True)
+            P.matmul(out, lay(m, par, 0), src[:, 0:64], True, False)
+            last = P.matmul(out, lay(m, par, 1), src[:, 64:128], False, True)
         return mark(last)
 
     def narrow(lst, t):
         return [mark(V.tensor_copy(lst[:, 4 * c:4 * c + 4], t[:, :, c])) for c in range(2)]
 
-    V.wait_ge(T.sem.sin, 2 * 16)
-    e_sf = mark(V.tensor_copy(T.splf[:, :], T.splc[:, :]))
+    V.wait_ge(T.sem.sin, 16)
+    e_sf = mark(V.tensor_copy(T.splf[0:64, :], T.splc[0:64, :]))
     need(V, e_sf)
-    V.wait_ge(T.sem.xin, 16 * 16)
-    e = mark(V.tensor_scalar(T.ge0[:, :], T.xq[:, :], T.splf[:, 0:1], None, Op.is_ge))
+    V.wait_ge(T.sem.cin, 8 * 16)
+    e = mark(V.tensor_scalar(T.ge0[0:64, :], T.xc[0:64, :], T.splf[0:64, 0:1], None, Op.is_ge))
     need(P, e_dm, e)
-    e_e = mark(P.matmul(T.pse[:, 0:128], T.hdm[:, :], T.ge0[:, :], True, True))
-    need(V, e_zer, e_init, e_e)
-    e = mark(V.tensor_tensor_scan(T.cnt[:, :], T.pse[:, 0:128], T.zer[:, :], T.init[:, 0:1], Op.add, Op.add))
+    e_e = mark(P.matmul(T.pse[0:64, 0:128], T.bdm[0:64, :], T.ge0[0:64, :], True, True))
+    need(V, e_q8)
+    e_qf = mark(V.tensor_copy(T.q8f[0:8, :], T.q8[0:8, :]))
+    need(P, e_rep, e_qf)
+    e_bc = mark(P.matmul(T.psx[:, 0:128], T.rep[0:8, :], T.q8f[0:8, :], True, True))
+    need(V, e_xs0, e_init, e_e)
+    e = mark(V.tensor_tensor_scan(T.cnt[0:64, :], T.pse[0:64, 0:128], T.xs[0:64, 0:128], T.init[0:64, 0:1], Op.add, Op.add))
     need(V, e)
-    e_p = mark(V.tensor_tensor(T.pslot[:, :], T.cnt[:, :], T.pse[:, 0:128], Op.mult))
-    need(P, e_lay, e_p)
-    e = lists(T.ps0, T.pslot)
-    need(V, e4)
-    e_dd = mark(V.tensor_copy(T.hdd[:, :], T.cdd[:, :]))
+    e_p = mark(V.tensor_tensor(T.pslot[0:64, :], T.cnt[0:64, :], T.pse[0:64, 0:128], Op.mult))
+    need(P, e_sl, e_p)
+    for par in range(2):
+        out = T.ps0[:, 0:4, 16 * par:16 * par + 16]
+        P.matmul(out, T.bsl[0:64, 128 * par + 8:128 * par + 136], T.pslot[0:64, 0:64], True, False)
+        last = P.matmul(out, T.bsl[0:64, 128 * par + 7:128 * par + 135], T.pslot[0:64, 64:128], False, True)
+    e = mark(last)
+    need(V, e_bc)
+    e_xq = mark(V.tensor_copy(T.xq[:, :], T.psx[:, 0:128]))
     need(V, e_beg)
     e_bl = mark(V.tensor_copy(T.begl[:, :], T.begi[:, :]))
     need(V, e)
     e = mark(V.transpose(T.tslot[:, :, :], T.ps0[:, 0:4, :]))
     need(V, e)
     es = narrow(T.lslot, T.tslot)
-    need(V, e_xs0, *es)
+    need(V, e_xq, *es)
     e_x = mark(V.tensor_copy(T.xs[:, 0:256].indirect(T.lslot[:, 0:8]), T.xq[:, :]))
 
     W = len(topo.engines(core, T.cores[(me + 1) % N])) // 4
@@ -195,9 +204,12 @@ def rank_program(g, core, T, topo):
 
     for par in range(2):
         for b in range(8):
-            last = P.matmul(T.pse[:, 256 + 16 * par:272 + 16 * par], lay(par, b), T.pslot[:, b:128:8], b == 0, b == 7)
+            last = P.matmul(T.pse[:, 256 + 16 * par:272 + 16 * par], T.bsl[0:64, 128 * par + 8 - b:128 * par + 136 - b],
+                            T.pslot[0:64, b:128:8], b == 0, b == 7)
     e_lb = mark(last)
 
+    need(V, e4)
+    e_dd = mark(V.tensor_copy(T.hdd[:, :], T.bdd[:, :]))
     need(V, e_bl)
     V.wait_ge(T.sem.kin, 16 * 16)
     e_k = [mark(V.tensor_copy(T["ckr%d" % h][:, :], T.kids[:, 0:4081].indirect(T.begl[:, 64 * h:64 * h + 64])))
@@ -219,8 +231,11 @@ def rank_program(g, core, T, topo):
         e_t.append(mark(S.activation(T.dck[:, 512 * q:512 * q + 512], T["pd%d" % q][:, :], Act.Copy)))
     need(V, e_nkc)
     e_n0 = mark(V.tensor_copy(T.nk0[:, :], T.nkc[:, 0:1]))
+    need(V, e_lay)
+    e_hl = mark(V.tensor_copy(T.hlay[:, :], T.blay[:, :]))
 
     need(V, e_n0, e_d0)
+    need(P, e_hl)
     lst = [None, None]
     e_l = [[], []]
     for l in range(1, 5):
@@ -251,10 +266,12 @@ def rank_program(g, core, T, topo):
         e_s = []
         for h in range(2):
             need(P, e_m[h])
-            e_s.append(lists(T["ps%d" % h], p[h]))
+            e_s.append(lists(T.hlay, T["ps%d" % h], p[h]))
         if l == 1:
             need(V, e_d[3])
-            e_t.append(mark(V.tensor_copy(T.dck[:, 1536:2048], T.pd3[:, :])))
+            e = mark(V.tensor_copy(T.dck[:, 1536:1792], T.pd3[:, 0:256]))
+            need(S, e)
+            e_t += [e, mark(S.activation(T.dck[:, 1792:2048], T.pd3[:, 256:512], Act.Copy))]
         e_r = []
         for h in range(2):
             need(V, e_s[h])
@@ -281,10 +298,13 @@ def rank_program(g, core, T, topo):
     e = mark(V.transpose(T.tback[:, :], T.pse[:, 256:288]))
     need(V, e)
     e = mark(V.tensor_copy(T.lback[:, :], T.tback[:, 0:8]))
-    need(V, e, e_ar)
-    V.wait_ge(T.sem.ra, 7 * W)
-    e = mark(V.tensor_copy(T.ysb[:, :], T.ar[:, 0:256].indirect(T.lback[:, 0:8])))
-    need(Y, e)
+    outs = []
+    for q, h in ((V, 0), (S, 1)):
+        need(q, e, e_ar)
+        q.wait_ge(T.sem.ra, 7 * W)
+        src, dst = T.ar[:, 0:256].indirect(T.lback[:, 4 * h:4 * h + 4]), T.ysb[:, 64 * h:64 * h + 64]
+        outs.append(mark(S.activation(dst, src, Act.Copy) if h else V.tensor_copy(dst, src)))
+    need(Y, *outs)
     e = mark(Y.dma_start(T.y[:, :], T.ysb[:, :]), 16)
     need(Y, e)
     g.wait_ge(T.sem.qs, 7 * W)

from concourse.bass import DstId, RemoteDMATransfer
from concourse.mybir import AluOpType as Op, ActivationFunctionType as Act

N = 8
NEV = 130
HALF = ((1, 2, 3, 4), (5, 6, 7))

SCRATCH = {
    "xc": ("sbuf", [128, 128], "int32"),
    "q8": ("sbuf", [128, 128], "int32"),
    "q8f": ("sbuf", [128, 128], "float32"),
    "xq": ("sbuf", [128, 128], "float32"),
    "splc": ("sbuf", [128, 1], "int32"),
    "splf": ("sbuf", [128, 1], "float32"),
    "pand": ("sbuf", [128, 1], "int32"),
    "init": ("sbuf", [128, 1], "float32"),
    "ge0": ("sbuf", [128, 128], "bfloat16"),
    "cnt": ("sbuf", [128, 128], "float32"),
    "pslot": ("sbuf", [128, 128], "bfloat16"),
    "tslot": ("sbuf", [128, 4, 32], "float32"),
    "lslot": ("sbuf", [128, 8], "uint16"),
    "tback": ("sbuf", [128, 32], "float32"),
    "lback": ("sbuf", [128, 8], "uint16"),
    "xs": ("sbuf", [128, 256], "float32"),
    "pg": ("sbuf", [128, 128], "int32"),
    "rep": ("sbuf", [128, 128], "float32"),
    "bdm": ("sbuf", [128, 64], "bfloat16"),
    "bsl": ("sbuf", [128, 264], "bfloat16"),
    "blay": ("sbuf", [128, 264], "bfloat16"),
    "bdd": ("sbuf", [128, 128], "bfloat16"),
    "hlay": ("sbuf", [128, 264], "float16"),
    "hdd": ("sbuf", [128, 128], "float16"),
    "kids": ("sbuf", [128, 4096], "int32"),
    "begi": ("sbuf", [128, 128], "int32"),
    "begl": ("sbuf", [128, 128], "uint16"),
    "ckr0": ("sbuf", [128, 1024], "float16"),
    "ckr1": ("sbuf", [128, 1024], "float16"),
    "dck": ("sbuf", [128, 2048], "float32"),
    "nkt": ("sbuf", [128, 2048], "int32"),
    "nkc": ("sbuf", [128, 8], "int32"),
    "nk0": ("sbuf", [128, 1], "float32"),
    "vect": ("sbuf", [128, 2048], "bfloat16"),
    "xr": ("sbuf", [128, 256], "float32"),
    "ans0": ("sbuf", [128, 128], "bfloat16"),
    "ans1": ("sbuf", [128, 128], "bfloat16"),
    "ar": ("sbuf", [128, 256], "bfloat16"),
    "ysb": ("sbuf", [128, 128], "bfloat16"),
    "pse": ("psum", [128, 512], "float32"),
    "psx": ("psum", [128, 512], "float32"),
    "ps0": ("psum", [128, 16, 32], "float32"),
    "ps1": ("psum", [128, 16, 32], "float32"),
}
for _q in range(4):
    SCRATCH["pd%d" % _q] = ("psum", [128, 512], "float32")
for _h in range(2):
    for _l in range(1, 5):
        SCRATCH["g%d_%d" % (_h, _l)] = ("sbuf", [128, 128], "float16")
        SCRATCH["p%d_%d" % (_h, _l)] = ("sbuf", [128, 128], "float16")
        SCRATCH["t%d_%d" % (_h, _l)] = ("sbuf", [128, 4, 32], "float32")
        SCRATCH["l%d_%d" % (_h, _l)] = ("sbuf", [128, 8], "uint16")

SEMAPHORES = ["qa", "qb", "qs", "ra", "rs", "sin", "cin", "kin", "gate"] + ["e%d" % i for i in range(NEV)]


def rank_program(g, core, T, topo):
    me = T.rank_of(core)
    if me is None:
        return
    V, S, P, Y = g.vector, g.scalar, g.tensor, g.sync
    used = [0]
    open_events = {}

    def mark(inst, n=1):
        i = used[0]
        used[0] += 1
        inst.then_inc(T.sem["e%d" % i], n)
        open_events[i] = n
        return i, n

    def need(queue, *events):
        for i, n in events:
            queue.wait_ge(T.sem["e%d" % i], n)
            open_events.pop(i, None)

    S.dma_start(T.splc[0:64, 0:1], T.spl[:, :]).then_inc(T.sem.sin, 16)
    for r in range(N):
        (Y, S)[r % 2].dma_start(T.xc[r:64:8, :], T.q[:, :]).then_inc(T.sem.cin, 16)
    e_q8 = mark(Y.dma_start(T.q8[0:8, :], T.q[:, :]), 16)
    e_beg = mark(Y.dma_start(T.begi[:, :], T.beg[:, :]), 16)
    for o in range(16):
        (S, Y)[o % 2].dma_start(T.kids[o:128:16, 0:4081], T.kid[:, o:o + 4081]).then_inc(T.sem.kin, 16)
    e_nkc = mark(Y.dma_start(T.nkc[:, :], T.nk[:, 0:8]), 16)
    Y.wait_ge(T.sem.gate, 1)
    e_nk = mark(Y.dma_start(T.nkt[:, :], T.nk[:, :]), 16)
    e_vec = mark(Y.dma_start(T.vect[:, :], T.vec[:, :]), 16)

    e_z1 = mark(V.memset(T.bdm[0:64, :], 0.0))
    e_z2 = mark(V.memset(T.bsl[:, :], 0.0))
    e_z3 = mark(V.memset(T.bdd[:, :], 0.0))
    e_z4 = mark(V.memset(T.blay[:, :], 0.0))
    e_xs0 = mark(V.memset(T.xs[:, :], 0.0))

    def sel(ap, pattern, cmp, fill, base, cm):
        return mark(g.affine_select(ap, ap, pattern, cmp, fill, base, cm))

    e_pg = mark(g.iota(T.pg[:, :], [[-1, 8], [0, 16]], 0, 1))
    need(g, e_z1)
    e1 = sel(T.bdm[0:64, :], [[-1, 64]], Op.not_equal, -1.0, -1, 1)
    need(g, e1)
    e1 = sel(T.bdm[0:64, 7:64:8], [[-8, 8]], Op.not_equal, 0.0, -8, 1)
    need(g, e1)
    e_dm = sel(T.bdm[0:64, :], [[-1, 64]], Op.not_equal, 1.0, 0, 1)
    need(g, e_z2)
    e2 = sel(T.bsl[:, 8:264:32], [[8, 2], [16, 4]], Op.is_gt, 1.0, 0, -1)
    need(g, e2)
    e_sl = sel(T.bsl[:, 8:264:32], [[8, 2], [16, 4]], Op.is_ge, 0.0, 7, -1)
    need(g, e_z3)
    e4 = sel(T.bdd[:, :], [[-1, 128]], Op.not_equal, -1.0, 1, 1)
    need(g, e4)
    e4 = sel(T.bdd[:, 0:128:16], [[-16, 8]], Op.not_equal, 0.0, 1, 1)
    need(g, e4)
    e4 = sel(T.bdd[:, :], [[-1, 128]], Op.not_equal, 1.0, 0, 1)
    need(g, e_z4)
    e5 = sel(T.blay[:, 8:264:32], [[16, 2], [32, 4]], Op.is_gt, 1.0, 0, -1)
    need(g, e5)
    e_lay = sel(T.blay[:, 8:264:32], [[16, 2], [32, 4]], Op.is_ge, 0.0, 15, -1)
    need(V, e_pg)
    e_rep = mark(V.tensor_scalar(T.rep[:, :], T.pg[:, :], 0.0, None, Op.is_equal))
    e_pa = mark(V.tensor_scalar(T.pand[0:64, :], T.pg[0:64, 0:1], 7, None, Op.bitwise_and))
    need(V, e_pa)
    e_init = mark(V.tensor_scalar(T.init[0:64, :], T.pand[0:64, :], 32.0, -1.0, Op.mult, Op.add))

    def lay(m, par, c):
        return m[:, 128 * par + 8 - c:128 * par + 136 - c]

    def lists(m, ps, src):
        for par in range(2):
            out = ps[:, 0:4, 16 * par:16 * par + 16]
            P.matmul(out, lay(m, par, 0), src[:, 0:64], True, False)
            last = P.matmul(out, lay(m, par, 1), src[:, 64:128], False, True)
        return mark(last)

    def narrow(lst, t):
        return [mark(V.tensor_copy(lst[:, 4 * c:4 * c + 4], t[:, :, c])) for c in range(2)]

    V.wait_ge(T.sem.sin, 16)
    e_sf = mark(V.tensor_copy(T.splf[0:64, :], T.splc[0:64, :]))
    need(V, e_sf)
    V.wait_ge(T.sem.cin, 8 * 16)
    e = mark(V.tensor_scalar(T.ge0[0:64, :], T.xc[0:64, :], T.splf[0:64, 0:1], None, Op.is_ge))
    need(P, e_dm, e)
    e_e = mark(P.matmul(T.pse[0:64, 0:128], T.bdm[0:64, :], T.ge0[0:64, :], True, True))
    need(V, e_q8)
    e_qf = mark(V.tensor_copy(T.q8f[0:8, :], T.q8[0:8, :]))
    need(P, e_rep, e_qf)
    e_bc = mark(P.matmul(T.psx[:, 0:128], T.rep[0:8, :], T.q8f[0:8, :], True, True))
    need(V, e_xs0, e_init, e_e)
    e = mark(V.tensor_tensor_scan(T.cnt[0:64, :], T.pse[0:64, 0:128], T.xs[0:64, 0:128], T.init[0:64, 0:1], Op.add, Op.add))
    need(V, e)
    e_p = mark(V.tensor_tensor(T.pslot[0:64, :], T.cnt[0:64, :], T.pse[0:64, 0:128], Op.mult))
    need(P, e_sl, e_p)
    for par in range(2):
        out = T.ps0[:, 0:4, 16 * par:16 * par + 16]
        P.matmul(out, T.bsl[0:64, 128 * par + 8:128 * par + 136], T.pslot[0:64, 0:64], True, False)
        last = P.matmul(out, T.bsl[0:64, 128 * par + 7:128 * par + 135], T.pslot[0:64, 64:128], False, True)
    e = mark(last)
    need(V, e_bc)
    e_xq = mark(V.tensor_copy(T.xq[:, :], T.psx[:, 0:128]))
    need(V, e_beg)
    e_bl = mark(V.tensor_copy(T.begl[:, :], T.begi[:, :]))
    need(V, e)
    e = mark(V.transpose(T.tslot[:, :, :], T.ps0[:, 0:4, :]))
    need(V, e)
    es = narrow(T.lslot, T.tslot)
    need(V, e_xq, *es)
    e_x = mark(V.tensor_copy(T.xs[:, 0:256].indirect(T.lslot[:, 0:8]), T.xq[:, :]))

    W = len(topo.engines(core, T.cores[(me + 1) % N])) // 4

    def send(ks, make, sem):
        tr = []
        for i, k in enumerate(ks):
            src, dst, to = make(k)
            c = T.cores[to]
            rid, pnc = topo.addr(c, core)
            m = 0
            for x in topo.engines(core, c)[W * i:W * i + W]:
                m |= 1 << x
            tr.append(RemoteDMATransfer(src=src, dst=dst, dst_ids=[DstId(rid=rid, pnc=pnc)], dma_engine_mask=m,
                                        remote_sem=sem))
        return tr

    def to_owner(k):
        d = (me + k) % N
        return T.xs[:, 32 * d:32 * d + 32], T.xr[:, 32 * k - 32:32 * k], d

    need(g, e_x)
    g.remote_dma_fused(send(HALF[0], to_owner, T.sem.qa), local_sem=T.sem.qs)
    g.sem_inc(T.sem.gate, 1)
    g.remote_dma_fused(send(HALF[1], to_owner, T.sem.qb), local_sem=T.sem.qs)

    need(S, e_x)
    e_own = mark(S.activation(T.xr[:, 224:256], T.xs[:, 32 * me:32 * me + 32], Act.Copy))

    for par in range(2):
        for b in range(8):
            last = P.matmul(T.pse[:, 256 + 16 * par:272 + 16 * par], T.bsl[0:64, 128 * par + 8 - b:128 * par + 136 - b],
                            T.pslot[0:64, b:128:8], b == 0, b == 7)
    e_lb = mark(last)

    need(V, e4)
    e_dd = mark(V.tensor_copy(T.hdd[:, :], T.bdd[:, :]))
    need(V, e_bl)
    V.wait_ge(T.sem.kin, 16 * 16)
    e_k = [mark(V.tensor_copy(T["ckr%d" % h][:, :], T.kids[:, 0:4081].indirect(T.begl[:, 64 * h:64 * h + 64])))
           for h in range(2)]
    need(P, e_dd, e_k[0])
    e_d0 = mark(P.matmul(T.pse[:, 320:321], T.hdd[:, :], T.ckr0[:, 0:1], True, True))
    e_d = []
    for h in range(2):
        if h:
            need(P, e_k[1])
        for a in range(16):
            c0 = 128 * (a % 4) + 64 * h
            last = P.matmul(T["pd%d" % (a // 4)][:, c0:c0 + 64], T.hdd[:, :], T["ckr%d" % h][:, a:1024:16], True, True)
            if h and a % 4 == 3:
                e_d.append(mark(last))
    e_t = []
    for q in range(3):
        need(S, e_d[q])
        e_t.append(mark(S.activation(T.dck[:, 512 * q:512 * q + 512], T["pd%d" % q][:, :], Act.Copy)))
    need(V, e_nkc)
    e_n0 = mark(V.tensor_copy(T.nk0[:, :], T.nkc[:, 0:1]))
    need(V, e_lay)
    e_hl = mark(V.tensor_copy(T.hlay[:, :], T.blay[:, :]))

    need(V, e_n0, e_d0)
    need(P, e_hl)
    lst = [None, None]
    e_l = [[], []]
    for l in range(1, 5):
        p = [T["p%d_%d" % (h, l)] for h in range(2)]
        x = [T.xr[:, 128 * h:128 * h + 128] for h in range(2)]
        e_m = []
        if l == 1:
            for h in range(2):
                if h == 0:
                    V.wait_ge(T.sem.qa, 4 * W)
                else:
                    need(V, e_own)
                    V.wait_ge(T.sem.qb, 3 * W)
                e_m.append(mark(V.tensor_scalar(p[h][:, :], x[h], T.nk0[:, 0:1], T.pse[:, 320:321], Op.is_ge, Op.mult)))
        else:
            if l == 2:
                need(V, e_nk)
            e_g = []
            for h in range(2):
                need(V, *e_l[h])
                e_g.append(mark(V.tensor_tensor(T["g%d_%d" % (h, l)][:, :], T.nkt[:, 0:2048].indirect(lst[h]), x[h], Op.is_le)))
            if l == 2:
                need(V, *e_t)
            for h in range(2):
                need(V, e_g[h])
                e_m.append(mark(V.tensor_tensor(p[h][:, :], T.dck[:, 0:2048].indirect(lst[h]),
                                                T["g%d_%d" % (h, l)][:, :], Op.mult)))
        e_s = []
        for h in range(2):
            need(P, e_m[h])
            e_s.append(lists(T.hlay, T["ps%d" % h], p[h]))
        if l == 1:
            need(V, e_d[3])
            e = mark(V.tensor_copy(T.dck[:, 1536:1792], T.pd3[:, 0:256]))
            need(S, e)
            e_t += [e, mark(S.activation(T.dck[:, 1792:2048], T.pd3[:, 256:512], Act.Copy))]
        e_r = []
        for h in range(2):
            need(V, e_s[h])
            e_r.append(mark(V.transpose(T["t%d_%d" % (h, l)][:, :, :], T["ps%d" % h][:, 0:4, :])))
        for h in range(2):
            need(V, e_r[h])
            e_l[h] = narrow(T["l%d_%d" % (h, l)], T["t%d_%d" % (h, l)])
            lst[h] = T["l%d_%d" % (h, l)][:, :]

    def to_asker(k):
        h, c = (k - 1) // 4, 32 * ((k - 1) % 4)
        return T["ans%d" % h][:, c:c + 32], T.ar[:, 32 * me:32 * me + 32], (me - k) % N

    need(V, e_vec)
    for h in range(2):
        need(V, *e_l[h])
        e_a = mark(V.tensor_copy(T["ans%d" % h][:, :], T.vect[:, 0:2048].indirect(lst[h])))
        need(g, e_a)
        g.remote_dma_fused(send(HALF[h], to_asker, T.sem.ra), local_sem=T.sem.rs)
    need(S, e_a)
    e_ar = mark(S.activation(T.ar[:, 32 * me:32 * me + 32], T.ans1[:, 96:128], Act.Copy))

    need(V, e_lb)
    e = mark(V.transpose(T.tback[:, :], T.pse[:, 256:288]))
    need(V, e)
    e = mark(V.tensor_copy(T.lback[:, :], T.tback[:, 0:8]))
    outs = []
    for q, h in ((V, 0), (S, 1)):
        need(q, e, e_ar)
        q.wait_ge(T.sem.ra, 7 * W)
        src, dst = T.ar[:, 0:256].indirect(T.lback[:, 4 * h:4 * h + 4]), T.ysb[:, 64 * h:64 * h + 64]
        outs.append(mark(S.activation(dst, src, Act.Copy) if h else V.tensor_copy(dst, src)))
    need(Y, *outs)
    e = mark(Y.dma_start(T.y[:, :], T.ysb[:, :]), 16)
    need(Y, e)
    g.wait_ge(T.sem.qs, 7 * W)
    g.wait_ge(T.sem.rs, 7 * W)
    for i in sorted(open_events):
        need(g, (i, open_events[i]))
